import numpy as np
import ml_dtypes

BF16 = ml_dtypes.bfloat16


def bf(x):
    return np.asarray(x, np.float32).astype(BF16)


def f32(x):
    return np.asarray(x, np.float32)


def f64(x):
    return np.asarray(x).astype(np.float64)


def striped(idx):
    return np.concatenate([l.reshape(-1, 16).T for l in idx])


def rows(idx, k):
    return np.tile(np.repeat(idx, 16, axis=0), (k // (16 * 8), 1))


def look(tab, idx):
    return np.take_along_axis(f64(tab), rows(idx, len(tab)), axis=1)


K, S, V, N, M = 128, 2048, 2048, 2048, 256


def setup_inputs():
    return {"tab": f32(0.5 * np.random.standard_normal((K, S))), "y": f32(np.random.standard_normal((K, V))), "w": bf(np.random.standard_normal((K, M)) / np.sqrt(K)), "offs": striped(np.stack([np.random.permutation(S)[:N] for _ in range(8)]))}


def reference(tab, y, w, offs):
    idx = np.stack([g.T.reshape(-1) for g in np.split(offs, 8)])
    t = look(tab, idx)
    x = np.exp(t) * f64(y)
    y = f64(w).T @ x
    return y

@@ -1,0 +1,52 @@
+import concourse.mybir as mybir
+
+F32 = mybir.dt.float32
+BF16 = mybir.dt.bfloat16
+U16 = mybir.dt.uint16
+EXP = mybir.ActivationFunctionType.Exp
+MULT = mybir.AluOpType.mult
+
+P = 128
+PIECE = 512
+GROUP = 16
+
+FLOPS = 2 * 128 * 256 * 2048
+
+
+def tile_lookup_gate_exp_none_kernel(tc, tab, y, w, offs, out):
+    nc = tc.nc
+    table_cols = tab.shape[1]
+    n = y.shape[1]
+    m = w.shape[1]
+    pieces = n // PIECE
+    blocks = m // P
+    with (
+        tc.tile_pool(name="held", bufs=1) as held,
+        tc.tile_pool(name="work", bufs=pieces) as work,
+        tc.tile_pool(name="staged", bufs=pieces * blocks) as staged,
+        tc.psum_pool(name="psum", bufs=pieces * blocks) as psum,
+    ):
+        offsets = held.tile([P, n // GROUP], U16, name="offsets")
+        table = held.tile([P, table_cols], F32, name="table")
+        weights = held.tile([P, m], BF16, name="weights")
+        nc.sync.dma_start(offsets[:], offs)
+        nc.sync.dma_start(table[:], tab)
+        nc.sync.dma_start(weights[:], w)
+        streams = []
+        for c in range(pieces):
+            stream = work.tile([P, PIECE], F32, name="stream")
+            nc.sync.dma_start(stream[:], y[:, c * PIECE : (c + 1) * PIECE])
+            streams.append(stream)
+        for c in range(pieces):
+            cols = slice(c * PIECE, (c + 1) * PIECE)
+            gate = work.tile([P, PIECE], F32, name="gate")
+            piece_offsets = offsets[:, c * PIECE // GROUP : (c + 1) * PIECE // GROUP]
+            nc.scalar.activation(gate[:], table[:].indirect(piece_offsets), EXP)
+            x = work.tile([P, PIECE], BF16, name="x")
+            nc.vector.tensor_tensor(x[:], gate[:], streams[c][:], MULT)
+            for b in range(blocks):
+                product = psum.tile([P, PIECE], F32, name="product")
+                nc.tensor.matmul(product[:], weights[:, b * P : (b + 1) * P], x[:], start=True, stop=True)
+                result = staged.tile([P, PIECE], F32, name="result")
+                nc.vector.tensor_copy(result[:], product[:])
+                nc.sync.dma_start(out[b * P : (b + 1) * P, cols], result[:])

@@ -9,6 +9,7 @@ MULT = mybir.AluOpType.mult
 P = 128
 PIECE = 512
 GROUP = 16
+WARM_MATMULS = 14
 
 FLOPS = 2 * 128 * 256 * 2048
 
@@ -20,9 +21,10 @@ def tile_lookup_gate_exp_none_kernel(tc, tab, y, w, offs, out):
     m = w.shape[1]
     pieces = n // PIECE
     blocks = m // P
+    columns = [slice(c * PIECE, (c + 1) * PIECE) for c in range(pieces)]
     with (
         tc.tile_pool(name="held", bufs=1) as held,
-        tc.tile_pool(name="work", bufs=pieces) as work,
+        tc.tile_pool(name="by_piece", bufs=pieces) as by_piece,
         tc.tile_pool(name="staged", bufs=pieces * blocks) as staged,
         tc.psum_pool(name="psum", bufs=pieces * blocks) as psum,
     ):
@@ -32,21 +34,35 @@ def tile_lookup_gate_exp_none_kernel(tc, tab, y, w, offs, out):
         nc.sync.dma_start(offsets[:], offs)
         nc.sync.dma_start(table[:], tab)
         nc.sync.dma_start(weights[:], w)
-        streams = []
+        streams = [by_piece.tile([P, PIECE], F32, name="stream") for c in range(pieces)]
         for c in range(pieces):
-            stream = work.tile([P, PIECE], F32, name="stream")
-            nc.sync.dma_start(stream[:], y[:, c * PIECE : (c + 1) * PIECE])
-            streams.append(stream)
+            nc.sync.dma_start(streams[c][:], y[:, columns[c]])
+
+        warm_in = held.tile([P, 8], F32, name="warm_in")
+        warm_out = held.tile([P, 8], F32, name="warm_out")
+        nc.vector.memset(warm_in[:], 0.0)
+        nc.scalar.activation(warm_out[:], warm_in[:], EXP)
+
+        zeros = held.tile([P, PIECE], BF16, name="zeros")
+        nc.gpsimd.memset(zeros[:], 0.0)
+        warm_product = psum.tile([P, PIECE], F32, name="product")
+        for step in range(WARM_MATMULS):
+            nc.tensor.matmul(warm_product[:], zeros[:, :P], zeros[:], start=True, stop=True)
+
+        gates = [by_piece.tile([P, PIECE], F32, name="gate") for c in range(pieces)]
         for c in range(pieces):
-            cols = slice(c * PIECE, (c + 1) * PIECE)
-            gate = work.tile([P, PIECE], F32, name="gate")
             piece_offsets = offsets[:, c * PIECE // GROUP : (c + 1) * PIECE // GROUP]
-            nc.scalar.activation(gate[:], table[:].indirect(piece_offsets), EXP)
-            x = work.tile([P, PIECE], BF16, name="x")
-            nc.vector.tensor_tensor(x[:], gate[:], streams[c][:], MULT)
+            nc.scalar.activation(gates[c][:], table[:].indirect(piece_offsets), EXP)
+        for c in range(pieces):
+            x = by_piece.tile([P, PIECE], BF16, name="x")
+            engine = nc.gpsimd if c == pieces - 2 else nc.vector
+            engine.tensor_tensor(x[:], gates[c][:], streams[c][:], MULT)
             for b in range(blocks):
                 product = psum.tile([P, PIECE], F32, name="product")
                 nc.tensor.matmul(product[:], weights[:, b * P : (b + 1) * P], x[:], start=True, stop=True)
                 result = staged.tile([P, PIECE], F32, name="result")
-                nc.vector.tensor_copy(result[:], product[:])
-                nc.sync.dma_start(out[b * P : (b + 1) * P, cols], result[:])
+                if c == pieces - 2 or (c == pieces - 1 and b == blocks - 1):
+                    nc.scalar.copy(result[:], product[:])
+                else:
+                    nc.vector.tensor_copy(result[:], product[:])
+                nc.sync.dma_start(out[b * P : (b + 1) * P, columns[c]], result[:])

import concourse.mybir as mybir

F32 = mybir.dt.float32
BF16 = mybir.dt.bfloat16
U16 = mybir.dt.uint16
EXP = mybir.ActivationFunctionType.Exp
MULT = mybir.AluOpType.mult

P = 128
PIECE = 512
GROUP = 16
WARM_MATMULS = 14

FLOPS = 2 * 128 * 256 * 2048


def tile_lookup_gate_exp_none_kernel(tc, tab, y, w, offs, out):
    nc = tc.nc
    table_cols = tab.shape[1]
    n = y.shape[1]
    m = w.shape[1]
    pieces = n // PIECE
    blocks = m // P
    columns = [slice(c * PIECE, (c + 1) * PIECE) for c in range(pieces)]
    with (
        tc.tile_pool(name="held", bufs=1) as held,
        tc.tile_pool(name="by_piece", bufs=pieces) as by_piece,
        tc.tile_pool(name="staged", bufs=pieces * blocks) as staged,
        tc.psum_pool(name="psum", bufs=pieces * blocks) as psum,
    ):
        offsets = held.tile([P, n // GROUP], U16, name="offsets")
        table = held.tile([P, table_cols], F32, name="table")
        weights = held.tile([P, m], BF16, name="weights")
        nc.sync.dma_start(offsets[:], offs)
        nc.sync.dma_start(table[:], tab)
        nc.sync.dma_start(weights[:], w)
        streams = [by_piece.tile([P, PIECE], F32, name="stream") for c in range(pieces)]
        for c in range(pieces):
            nc.sync.dma_start(streams[c][:], y[:, columns[c]])

        warm_in = held.tile([P, 8], F32, name="warm_in")
        warm_out = held.tile([P, 8], F32, name="warm_out")
        nc.vector.memset(warm_in[:], 0.0)
        nc.scalar.activation(warm_out[:], warm_in[:], EXP)

        zeros = held.tile([P, PIECE], BF16, name="zeros")
        nc.gpsimd.memset(zeros[:], 0.0)
        warm_product = psum.tile([P, PIECE], F32, name="product")
        for step in range(WARM_MATMULS):
            nc.tensor.matmul(warm_product[:], zeros[:, :P], zeros[:], start=True, stop=True)

        gates = [by_piece.tile([P, PIECE], F32, name="gate") for c in range(pieces)]
        for c in range(pieces):
            piece_offsets = offsets[:, c * PIECE // GROUP : (c + 1) * PIECE // GROUP]
            nc.scalar.activation(gates[c][:], table[:].indirect(piece_offsets), EXP)
        for c in range(pieces):
            x = by_piece.tile([P, PIECE], BF16, name="x")
            engine = nc.gpsimd if c == pieces - 2 else nc.vector
            engine.tensor_tensor(x[:], gates[c][:], streams[c][:], MULT)
            for b in range(blocks):
                product = psum.tile([P, PIECE], F32, name="product")
                nc.tensor.matmul(product[:], weights[:, b * P : (b + 1) * P], x[:], start=True, stop=True)
                result = staged.tile([P, PIECE], F32, name="result")
                if c == pieces - 2 or (c == pieces - 1 and b == blocks - 1):
                    nc.scalar.copy(result[:], product[:])
                else:
                    nc.vector.tensor_copy(result[:], product[:])
                nc.sync.dma_start(out[b * P : (b + 1) * P, columns[c]], result[:])
